import numpy as np
import ml_dtypes


def mxq(x, axis, fmt="e4m3"):
    dtype, down = {"e4m3": (ml_dtypes.float8_e4m3fn, 7), "e5m2": (ml_dtypes.float8_e5m2, 14)}[fmt]
    v = np.moveaxis(np.asarray(x, np.float32).astype(ml_dtypes.bfloat16).astype(np.float64), axis, -1)
    blocks = v.reshape(v.shape[:-1] + (-1, 32))
    amax = np.abs(blocks).max(-1, keepdims=True)
    byte = np.maximum(np.where(amax > 0, np.frexp(amax)[1] - 1 + 127, 0) - down, 1)
    scale = np.exp2(byte - 127.0)
    codes = (blocks / scale).astype(np.float32).astype(dtype).astype(np.float64)
    return np.moveaxis((codes * scale).reshape(v.shape), -1, axis)


WIDE = False


def mx_kscale(k):
    if not WIDE:
        return np.ones(k)
    levels = np.array([24, -24, 12, -12, 0])
    if k % 512:
        return np.exp2(np.random.permutation(np.resize(levels, k // 32))).repeat(32)
    a = np.empty((k // 512, 16))
    for p in range(k // 512):
        a[p, :8] = np.random.permutation(np.resize(levels, 8))
        for g in range(8):
            far = levels[np.abs(levels - a[p, g]) >= 10]
            a[p, g + 8] = far[np.random.randint(len(far))]
    return np.exp2(a.ravel()).repeat(32)


def f64(x):
    return np.asarray(x).astype(np.float64)


def striped8(idx):
    return np.concatenate([v.reshape(-1, 16).T for v in idx]).astype(np.uint16)


def unstriped8(offs):
    return np.stack([offs[16 * g:16 * g + 16].T.reshape(-1) for g in range(8)]).astype(np.int64)


E2M1 = np.array([0.0, 0.5, 1.0, 1.5, 2.0, 3.0, 4.0, 6.0, -0.0, -0.5, -1.0, -1.5, -2.0, -3.0, -4.0, -6.0])


def pack_weight(w, fmt):
    k, n = w.shape
    w = f64(np.asarray(w, np.float32).astype(ml_dtypes.bfloat16)).reshape(k // 32, 32, n)
    amax = np.abs(w).max(1)
    if fmt == "e4m3":
        byte = np.frexp(amax)[1] - 1 + 127 - 7
    else:
        mant, ex = np.frexp(amax / 6.0)
        byte = np.where(mant > 0.5, ex, ex - 1) + 127
    byte = np.clip(np.where(amax > 0, byte, 1), 1, 254)
    scaled = (w * np.exp2(127.0 - byte)[:, None, :]).reshape(k, n).astype(np.float32)
    by_word = np.ascontiguousarray(scaled.reshape(k // 512, 128, 4, n).transpose(0, 1, 3, 2))
    if fmt == "e4m3":
        words = by_word.astype(ml_dtypes.float8_e4m3fn).view(np.uint8)
    else:
        c = by_word.astype(ml_dtypes.float4_e2m1fn).view(np.uint8) & 0xF
        words = (c[..., 0::2] | (c[..., 1::2] << 4)).reshape(k // 512, 128, 2 * n)
    return np.ascontiguousarray(words), np.ascontiguousarray(byte.astype(np.uint8).reshape(k // 512, 16, n))


def unpack_weight(words, scales, fmt):
    g, _, n = scales.shape
    words = np.ascontiguousarray(words).reshape(g, 128, n, -1)
    if fmt == "e4m3":
        vals = words.view(ml_dtypes.float8_e4m3fn).astype(np.float64)
    else:
        nib = np.empty((g, 128, n, 4), np.uint8)
        nib[..., 0::2] = words & 0xF
        nib[..., 1::2] = words >> 4
        vals = E2M1[nib]
    vals = vals * np.repeat(np.exp2(scales.astype(np.float64) - 127.0), 8, axis=1)[..., None]
    return vals.transpose(0, 1, 3, 2).reshape(g * 512, n)


def split(x):
    m, e = np.frexp(f64(x))
    hi = np.ldexp(np.trunc(16.0 * m) / 16.0, e)
    return hi, f64(x) - hi


def gelu(f):
    return 0.5 * f * (1.0 + np.tanh(np.sqrt(2.0 / np.pi) * (f + 0.044715 * f**3)))


K, L, N, T, J = 512, 512, 512, 2048, 1024


def setup_inputs():
    n = np.random.standard_normal
    s = mx_kscale(K)[:, None]
    s2 = mx_kscale(L)[:, None]
    p_wa = pack_weight(n((K, N)) / np.sqrt(K) / s, "e4m3")
    return {
        "xT": (n((K, T)) * s).astype(np.float32),
        "wgt": np.repeat(np.random.uniform(0.5, 2.0, (8, J)), 16, axis=0).astype(np.float32),
        "zT": (n((L, T)) * s2).astype(np.float32),
        "wgt2": np.repeat(np.random.uniform(0.5, 2.0, (8, J)), 16, axis=0).astype(np.float32),
        "wa_words": p_wa[0],
        "wa_scales": p_wa[1],
        "wb": (n((L, N)) / np.sqrt(L) / s2).astype(np.float32),
        "b": (0.3 * n(N)).astype(np.float32),
        "offs": striped8(np.stack([np.random.permutation(T)[:J] for _ in range(8)])),
        "offs2": striped8(np.stack([np.random.permutation(T)[:J] for _ in range(8)])),
    }


def reference(xT, wgt, zT, wgt2, wa_words, wa_scales, wb, b, offs, offs2):
    idx = unstriped8(offs)
    idx2 = unstriped8(offs2)
    rows = np.arange(K)
    xg = f64(wgt)[rows // 4 % 128] * f64(xT)[rows[:, None], idx[rows % 512 // 64]]
    xT_ = mxq(xg, 0, "e4m3")
    rows = np.arange(L)
    xg = f64(wgt2)[rows // 4 % 128] * f64(zT)[rows[:, None], idx2[rows % 512 // 64]]
    zT_ = mxq(xg, 0, "e4m3")
    wa_ = unpack_weight(wa_words, wa_scales, "e4m3")
    wb_hi, wb_lo = split(wb)
    wb_hi_, wb_lo_ = mxq(wb_hi, 0, "e4m3"), mxq(wb_lo, 0, "e4m3")
    ya = wa_.T @ xT_
    yb = wb_hi_.T @ zT_ + wb_lo_.T @ zT_
    return gelu(ya * yb + f64(b)[:, None])

@@ -1,0 +1,183 @@
+from contextlib import ExitStack
+
+import concourse.mybir as mybir
+
+K, L, N, T, J = 512, 512, 512, 2048, 1024
+FLOPS = 2 * (K + 2 * L) * N * J
+
+F32 = mybir.dt.float32
+BF16 = mybir.dt.bfloat16
+I32 = mybir.dt.int32
+U32 = mybir.dt.uint32
+U16 = mybir.dt.uint16
+U8 = mybir.dt.uint8
+FP8X4 = mybir.dt.float8_e4m3fn_x4
+ALU = mybir.AluOpType
+GELU = mybir.ActivationFunctionType.Gelu_apprx_tanh
+
+P = 128
+PACK = 4
+GROUP = 16
+BANK = 512
+HI_MASK = -(1 << 20)
+W_COLS = 256
+Z_COLS = 512
+X_COLS = 256
+
+
+def weave(engine_copy, woven, planes):
+    engine_copy(
+        woven.rearrange("p (c i) t -> p c t i", i=4),
+        planes.rearrange("p t (c i) -> p c t i", i=4),
+    )
+
+
+def tile_list_hl_mul_gelu_kernel(
+    tc, xT, wgt, zT, wgt2, wa_words, wa_scales, wb, b, offs, offs2, out
+):
+    nc = tc.nc
+    with ExitStack() as ctx:
+        keep = ctx.enter_context(tc.tile_pool(name="keep", bufs=1))
+        ring = ctx.enter_context(tc.tile_pool(name="ring", bufs=4))
+        psum = ctx.enter_context(tc.psum_pool(name="psum", bufs=8))
+
+        x_list = keep.tile([P, J // GROUP], U16, name="x_list")
+        z_list = keep.tile([P, J // GROUP], U16, name="z_list")
+        x_wgt = keep.tile([P, J], F32, name="x_wgt")
+        z_wgt = keep.tile([P, J], F32, name="z_wgt")
+        x_planes = [keep.tile([P, T], F32, name=f"x_plane{i}") for i in range(PACK)]
+        z_planes = [keep.tile([P, T], F32, name=f"z_plane{i}") for i in range(PACK)]
+        wb_raw = [keep.tile([P, PACK, W_COLS], F32, name=f"wb_raw{h}") for h in range(N // W_COLS)]
+        wa_codes = keep.tile([P, N], U32, name="wa_codes", align_bytes=64)
+        wa_plane = keep.tile([P, N], U8, name="wa_plane", align_bytes=64)
+        bias = keep.tile([P, N // P], F32, name="bias")
+
+        nc.gpsimd.memset(wa_plane[:].bitcast(I32), 0)
+
+        xT_planes = xT.rearrange("(p i) t -> p i t", i=PACK)
+        zT_planes = zT.rearrange("(p i) t -> p i t", i=PACK)
+        wb_planes = wb.rearrange("(p i) n -> p i n", i=PACK)
+        for h in range(N // W_COLS):
+            nc.sync.dma_start(wb_raw[h][:], wb_planes[:, :, h * W_COLS : (h + 1) * W_COLS])
+        nc.sync.dma_start(z_list[:], offs2)
+        nc.sync.dma_start(z_wgt[:], wgt2)
+        for i in range(PACK):
+            nc.sync.dma_start(z_planes[i][:], zT_planes[:, i, :])
+        nc.sync.dma_start(x_list[:], offs)
+        nc.sync.dma_start(x_wgt[:], wgt)
+        nc.sync.dma_start(x_planes[0][:], xT_planes[:, 0, :])
+        scale_rows = wa_scales[0].bitcast(I32)
+        for q in range(4):
+            nc.sync.dma_start(wa_plane[32 * q : 32 * q + 4, :].bitcast(I32), scale_rows[4 * q : 4 * q + 4, :])
+        nc.sync.dma_start(x_planes[1][:], xT_planes[:, 1, :])
+        with nc.allow_non_contiguous_dma(reason="one bias value a partition"):
+            nc.sync.dma_start(bias[:], b.rearrange("(m p) -> p m", p=P))
+        nc.sync.dma_start(wa_codes[:].bitcast(I32), wa_words[0].rearrange("p n i -> p (n i)").bitcast(I32))
+        nc.sync.dma_start(x_planes[2][:], xT_planes[:, 2, :])
+        nc.sync.dma_start(x_planes[3][:], xT_planes[:, 3, :])
+
+        wb_codes, wb_plane = [], []
+        wb_woven = []
+        for h in range(N // W_COLS):
+            hi = keep.tile([P, PACK, W_COLS], F32, name=f"hi{h}")
+            lo = keep.tile([P, PACK, W_COLS], F32, name=f"lo{h}")
+            woven = keep.tile([P, 2, W_COLS, PACK], BF16, name=f"wb_woven{h}", align_bytes=64)
+            nc.vector.tensor_scalar(hi[:].bitcast(I32), wb_raw[h][:].bitcast(I32), HI_MASK, None, ALU.bitwise_and)
+            nc.vector.tensor_tensor(lo[:], wb_raw[h][:], hi[:], ALU.subtract)
+            weave(nc.scalar.copy, woven[:, 0], hi[:])
+            weave(nc.scalar.copy, woven[:, 1], lo[:])
+            wb_woven.append(woven)
+        for h in range(N // W_COLS):
+            codes = keep.tile([P, 2 * W_COLS], U32, name=f"wb_codes{h}", align_bytes=64)
+            plane = keep.tile([P, 2 * W_COLS], U8, name=f"wb_plane{h}", align_bytes=64)
+            nc.vector.quantize_mx(
+                out=codes[:].bitcast(FP8X4), scales=plane[:], in_=wb_woven[h][:].rearrange("p s n t -> p (s n t)")
+            )
+            wb_codes.append(codes)
+            wb_plane.append(plane)
+
+        def gather(picked, planes, lists, weights, i, lo_col, cols):
+            nc.vector.tensor_tensor(
+                picked[:, i, lo_col : lo_col + cols],
+                planes[i][:].indirect(lists[:, lo_col // GROUP : (lo_col + cols) // GROUP]),
+                weights[:, lo_col : lo_col + cols],
+                ALU.mult,
+            )
+
+        def quantise(picked, lo_col, cols, tag):
+            woven = keep.tile([P, cols, PACK], BF16, name=f"woven_{tag}", align_bytes=64)
+            codes = keep.tile([P, cols], U32, name=f"codes_{tag}", align_bytes=64)
+            plane = keep.tile([P, cols], U8, name=f"plane_{tag}", align_bytes=64)
+            weave(nc.scalar.copy, woven[:], picked[:, :, lo_col : lo_col + cols])
+            nc.vector.quantize_mx(out=codes[:].bitcast(FP8X4), scales=plane[:], in_=woven[:].rearrange("p j t -> p (j t)"))
+            return codes, plane
+
+        z_picked = keep.tile([P, PACK, J], F32, name="z_picked")
+        for i in range(PACK - 1):
+            gather(z_picked, z_planes, z_list, z_wgt, i, 0, J)
+        for h in range(J // Z_COLS):
+            gather(z_picked, z_planes, z_list, z_wgt, PACK - 1, h * Z_COLS, Z_COLS)
+
+        x_picked = keep.tile([P, PACK, J], F32, name="x_picked")
+        yb = []
+        for h in range(J // Z_COLS):
+            gather(x_picked, x_planes, x_list, x_wgt, h, 0, J)
+            codes, plane = quantise(z_picked, h * Z_COLS, Z_COLS, f"z{h}")
+            sums = keep.tile([P, N // P, Z_COLS], F32, name=f"yb{h}")
+            for m in range(N // P):
+                bank = psum.tile([P, BANK], F32, name="bank")
+                half, at = divmod(m * P, W_COLS)
+                for part in range(2):
+                    cols = slice(part * W_COLS + at, part * W_COLS + at + P)
+                    nc.tensor.matmul_mx(
+                        out=bank[:],
+                        lhsT=wb_codes[half][:, cols].bitcast(FP8X4),
+                        lhsT_scale=wb_plane[half][:, cols],
+                        rhs=codes[:].bitcast(FP8X4),
+                        rhs_scale=plane[:],
+                        start=(part == 0),
+                        stop=(part == 1),
+                    )
+                nc.scalar.copy(sums[:, m, :], bank[:])
+            yb.append(sums)
+
+        gather(x_picked, x_planes, x_list, x_wgt, 2, 0, J)
+        chunks = J // X_COLS
+        out_rows = out.rearrange("(m p) j -> p m j", p=P)
+        per_bank = BANK // X_COLS
+        ready = {}
+
+        def finish(c):
+            codes, plane = ready[c]
+            half, at = divmod(c * X_COLS, Z_COLS)
+            for pair in range(N // P // per_bank):
+                bank = psum.tile([P, per_bank, X_COLS], F32, name="bank")
+                for u in range(per_bank):
+                    m = pair * per_bank + u
+                    nc.tensor.matmul_mx(
+                        out=bank[:, u, :],
+                        lhsT=wa_codes[:, m * P : (m + 1) * P].bitcast(FP8X4),
+                        lhsT_scale=wa_plane[:, m * P : (m + 1) * P],
+                        rhs=codes[:].bitcast(FP8X4),
+                        rhs_scale=plane[:],
+                        start=True,
+                        stop=True,
+                    )
+                rows = slice(pair * per_bank, (pair + 1) * per_bank)
+                product = ring.tile([P, per_bank, X_COLS], F32, name="product")
+                result = ring.tile([P, per_bank, X_COLS], F32, name="result")
+                nc.vector.tensor_tensor(product[:], bank[:], yb[half][:, rows, at : at + X_COLS], ALU.mult)
+                for u in range(per_bank):
+                    m = pair * per_bank + u
+                    nc.scalar.activation(result[:, u, :], product[:, u, :], GELU, bias=bias[:, m : m + 1])
+                nc.sync.dma_start(out_rows[:, rows, c * X_COLS : (c + 1) * X_COLS], result[:])
+
+        for c in range(chunks):
+            gather(x_picked, x_planes, x_list, x_wgt, PACK - 1, c * X_COLS, X_COLS)
+            if c >= 1:
+                ready[c - 1] = quantise(x_picked, (c - 1) * X_COLS, X_COLS, f"x{c - 1}")
+            if c >= 2:
+                finish(c - 2)
+        ready[chunks - 1] = quantise(x_picked, (chunks - 1) * X_COLS, X_COLS, f"x{chunks - 1}")
+        finish(chunks - 2)
+        finish(chunks - 1)

@@ -1,6 +1,7 @@
 from contextlib import ExitStack
 
 import concourse.mybir as mybir
+from concourse.masks import make_identity
 
 K, L, N, T, J = 512, 512, 512, 2048, 1024
 FLOPS = 2 * (K + 2 * L) * N * J
@@ -13,6 +14,7 @@ U16 = mybir.dt.uint16
 U8 = mybir.dt.uint8
 FP8X4 = mybir.dt.float8_e4m3fn_x4
 ALU = mybir.AluOpType
+COPY = mybir.ActivationFunctionType.Copy
 GELU = mybir.ActivationFunctionType.Gelu_apprx_tanh
 
 P = 128
@@ -20,9 +22,12 @@ PACK = 4
 GROUP = 16
 BANK = 512
 HI_MASK = -(1 << 20)
+SIGN_BIT = -(1 << 31)
 W_COLS = 256
-Z_COLS = 512
-X_COLS = 256
+HALF = 512
+CHUNKS = [512,256,256]
+Z_FIRST = 896
+X_EARLY = 768
 
 
 def weave(engine_copy, woven, planes):
@@ -38,7 +43,7 @@ def tile_list_hl_mul_gelu_kernel(
     nc = tc.nc
     with ExitStack() as ctx:
         keep = ctx.enter_context(tc.tile_pool(name="keep", bufs=1))
-        ring = ctx.enter_context(tc.tile_pool(name="ring", bufs=4))
+        ring = ctx.enter_context(tc.tile_pool(name="ring", bufs=8))
         psum = ctx.enter_context(tc.psum_pool(name="psum", bufs=8))
 
         x_list = keep.tile([P, J // GROUP], U16, name="x_list")
@@ -46,13 +51,19 @@ def tile_list_hl_mul_gelu_kernel(
         x_wgt = keep.tile([P, J], F32, name="x_wgt")
         z_wgt = keep.tile([P, J], F32, name="z_wgt")
         x_planes = [keep.tile([P, T], F32, name=f"x_plane{i}") for i in range(PACK)]
-        z_planes = [keep.tile([P, T], F32, name=f"z_plane{i}") for i in range(PACK)]
+        z_planes = [keep.tile([P, T], F32, name=f"z_plane{i}", align_bytes=64) for i in range(PACK)]
         wb_raw = [keep.tile([P, PACK, W_COLS], F32, name=f"wb_raw{h}") for h in range(N // W_COLS)]
         wa_codes = keep.tile([P, N], U32, name="wa_codes", align_bytes=64)
         wa_plane = keep.tile([P, N], U8, name="wa_plane", align_bytes=64)
         bias = keep.tile([P, N // P], F32, name="bias")
 
+        identity = keep.tile([P, P], F32, name="identity")
+        make_identity(nc, identity[:])
         nc.gpsimd.memset(wa_plane[:].bitcast(I32), 0)
+        warm = keep.tile([P, 1], F32, name="warm")
+        warm_out = keep.tile([P, 1], F32, name="warm_out")
+        nc.gpsimd.memset(warm[:], 0.0)
+        nc.scalar.activation(warm_out[:], warm[:], GELU)
 
         xT_planes = xT.rearrange("(p i) t -> p i t", i=PACK)
         zT_planes = zT.rearrange("(p i) t -> p i t", i=PACK)
@@ -60,79 +71,107 @@ def tile_list_hl_mul_gelu_kernel(
         for h in range(N // W_COLS):
             nc.sync.dma_start(wb_raw[h][:], wb_planes[:, :, h * W_COLS : (h + 1) * W_COLS])
         nc.sync.dma_start(z_list[:], offs2)
-        nc.sync.dma_start(z_wgt[:], wgt2)
+        nc.sync.dma_start(z_wgt[:, :Z_FIRST], wgt2[:, :Z_FIRST])
         for i in range(PACK):
             nc.sync.dma_start(z_planes[i][:], zT_planes[:, i, :])
+        nc.sync.dma_start(z_wgt[:, Z_FIRST:], wgt2[:, Z_FIRST:])
         nc.sync.dma_start(x_list[:], offs)
-        nc.sync.dma_start(x_wgt[:], wgt)
-        nc.sync.dma_start(x_planes[0][:], xT_planes[:, 0, :])
+        nc.sync.dma_start(x_wgt[:, :X_EARLY], wgt[:, :X_EARLY])
+        for i in range(PACK):
+            nc.sync.dma_start(x_planes[i][:], xT_planes[:, i, :])
+        nc.sync.dma_start(x_wgt[:, X_EARLY:], wgt[:, X_EARLY:])
+        nc.sync.dma_start(wa_codes[:].bitcast(I32), wa_words[0].rearrange("p n i -> p (n i)").bitcast(I32))
         scale_rows = wa_scales[0].bitcast(I32)
         for q in range(4):
             nc.sync.dma_start(wa_plane[32 * q : 32 * q + 4, :].bitcast(I32), scale_rows[4 * q : 4 * q + 4, :])
-        nc.sync.dma_start(x_planes[1][:], xT_planes[:, 1, :])
         with nc.allow_non_contiguous_dma(reason="one bias value a partition"):
             nc.sync.dma_start(bias[:], b.rearrange("(m p) -> p m", p=P))
-        nc.sync.dma_start(wa_codes[:].bitcast(I32), wa_words[0].rearrange("p n i -> p (n i)").bitcast(I32))
-        nc.sync.dma_start(x_planes[2][:], xT_planes[:, 2, :])
-        nc.sync.dma_start(x_planes[3][:], xT_planes[:, 3, :])
 
-        wb_codes, wb_plane = [], []
-        wb_woven = []
+        def quantise(woven, tag, slot=None):
+            words = woven.shape[1] // PACK
+            codes = keep.tile([P, words], U32, name=f"codes_{tag}", tag=slot or f"codes_{tag}", align_bytes=64)
+            plane = keep.tile([P, words], U8, name=f"plane_{tag}", align_bytes=64)
+            nc.vector.quantize_mx(out=codes[:].bitcast(FP8X4), scales=plane[:], in_=woven)
+            return codes, plane
+
+        hi_woven = keep.tile([P, N, PACK], BF16, name="hi_woven", align_bytes=64)
+        lo_woven = keep.tile([P, N, PACK], BF16, name="lo_woven", align_bytes=64)
+        minus_hi = []
         for h in range(N // W_COLS):
-            hi = keep.tile([P, PACK, W_COLS], F32, name=f"hi{h}")
-            lo = keep.tile([P, PACK, W_COLS], F32, name=f"lo{h}")
-            woven = keep.tile([P, 2, W_COLS, PACK], BF16, name=f"wb_woven{h}", align_bytes=64)
-            nc.vector.tensor_scalar(hi[:].bitcast(I32), wb_raw[h][:].bitcast(I32), HI_MASK, None, ALU.bitwise_and)
-            nc.vector.tensor_tensor(lo[:], wb_raw[h][:], hi[:], ALU.subtract)
-            weave(nc.scalar.copy, woven[:, 0], hi[:])
-            weave(nc.scalar.copy, woven[:, 1], lo[:])
-            wb_woven.append(woven)
-        for h in range(N // W_COLS):
-            codes = keep.tile([P, 2 * W_COLS], U32, name=f"wb_codes{h}", align_bytes=64)
-            plane = keep.tile([P, 2 * W_COLS], U8, name=f"wb_plane{h}", align_bytes=64)
-            nc.vector.quantize_mx(
-                out=codes[:].bitcast(FP8X4), scales=plane[:], in_=wb_woven[h][:].rearrange("p s n t -> p (s n t)")
+            negated = keep.tile([P, PACK, W_COLS], F32, name=f"minus_hi{h}")
+            nc.vector.tensor_scalar(
+                negated[:].bitcast(I32), wb_raw[h][:].bitcast(I32), HI_MASK, SIGN_BIT, ALU.bitwise_and, ALU.bitwise_xor
             )
-            wb_codes.append(codes)
-            wb_plane.append(plane)
+            weave(
+                lambda woven, planes: nc.scalar.activation(woven, planes, COPY, scale=-1.0),
+                hi_woven[:, h * W_COLS : (h + 1) * W_COLS, :],
+                negated[:],
+            )
+            minus_hi.append(negated)
+        wb_mx = [quantise(hi_woven[:].rearrange("p n t -> p (n t)"), "hi")]
+        lo_words = lo_woven[:].rearrange("p n t -> p (n t)").bitcast(F32).rearrange("p (n u) -> p n u", u=2)
+        for h in range(N // W_COLS):
+            turned = []
+            for at in range(0, W_COLS, P):
+                bank = psum.tile([P, PACK, P], F32, name="bank")
+                for i in range(PACK):
+                    for term, first in ((wb_raw[h], True), (minus_hi[h], False)):
+                        nc.tensor.matmul(
+                            bank[:, i, :], term[:, i, at : at + P], identity[:],
+                            start=first, stop=not first, is_transpose=True,
+                        )
+                pairs = keep.tile([P, 2, P, 2], BF16, name=f"lo_turned{h}_{at}")
+                nc.scalar.copy(pairs[:], bank[:].rearrange("n (u e) p -> n u p e", e=2))
+                turned.append(pairs)
+            bank = psum.tile([P, W_COLS // P, 2, P], F32, name="bank")
+            for block, pairs in enumerate(turned):
+                words = pairs[:].rearrange("n u p e -> n (u p e)").bitcast(F32)
+                for u in range(2):
+                    nc.tensor.transpose(bank[:, block, u, :], words[:, u * P : (u + 1) * P], identity[:])
+            nc.scalar.copy(
+                lo_words[:, h * W_COLS : (h + 1) * W_COLS, :].rearrange("p (m n) u -> p m n u", n=P),
+                bank[:].rearrange("p m u n -> p m n u"),
+            )
 
-        def gather(picked, planes, lists, weights, i, lo_col, cols):
+        def gather(picked, plane, lists, weights, start):
+            cols = picked.shape[1]
             nc.vector.tensor_tensor(
-                picked[:, i, lo_col : lo_col + cols],
-                planes[i][:].indirect(lists[:, lo_col // GROUP : (lo_col + cols) // GROUP]),
-                weights[:, lo_col : lo_col + cols],
+                picked,
+                plane[:].indirect(lists[:, start // GROUP : (start + cols) // GROUP]),
+                weights[:, start : start + cols],
                 ALU.mult,
             )
 
-        def quantise(picked, lo_col, cols, tag):
-            woven = keep.tile([P, cols, PACK], BF16, name=f"woven_{tag}", align_bytes=64)
-            codes = keep.tile([P, cols], U32, name=f"codes_{tag}", align_bytes=64)
-            plane = keep.tile([P, cols], U8, name=f"plane_{tag}", align_bytes=64)
-            weave(nc.scalar.copy, woven[:], picked[:, :, lo_col : lo_col + cols])
-            nc.vector.quantize_mx(out=codes[:].bitcast(FP8X4), scales=plane[:], in_=woven[:].rearrange("p j t -> p (j t)"))
-            return codes, plane
+        def weave_and_quantise(picked, tag):
+            woven = keep.tile([P, picked.shape[2], PACK], BF16, name=f"woven_{tag}", align_bytes=64)
+            weave(nc.scalar.copy, woven[:], picked)
+            return quantise(woven[:].rearrange("p j t -> p (j t)"), tag)
 
+        halves = range(J // HALF)
         z_picked = keep.tile([P, PACK, J], F32, name="z_picked")
+        x_early = keep.tile([P, PACK, X_EARLY], F32, name="x_early")
+        x_late = keep.tile([P, PACK, J - X_EARLY], F32, name="x_late")
         for i in range(PACK - 1):
-            gather(z_picked, z_planes, z_list, z_wgt, i, 0, J)
-        for h in range(J // Z_COLS):
-            gather(z_picked, z_planes, z_list, z_wgt, PACK - 1, h * Z_COLS, Z_COLS)
+            gather(z_picked[:, i, :Z_FIRST], z_planes[i], z_list, z_wgt, 0)
+        gather(z_picked[:, PACK - 1, :HALF], z_planes[PACK - 1], z_list, z_wgt, 0)
+        for i in range(PACK - 1):
+            gather(z_picked[:, i, Z_FIRST:], z_planes[i], z_list, z_wgt, Z_FIRST)
+        gather(z_picked[:, PACK - 1, HALF:], z_planes[PACK - 1], z_list, z_wgt, HALF)
+        wb_mx.append(quantise(lo_woven[:].rearrange("p n t -> p (n t)"), "lo", "z_plane0"))
 
-        x_picked = keep.tile([P, PACK, J], F32, name="x_picked")
         yb = []
-        for h in range(J // Z_COLS):
-            gather(x_picked, x_planes, x_list, x_wgt, h, 0, J)
-            codes, plane = quantise(z_picked, h * Z_COLS, Z_COLS, f"z{h}")
-            sums = keep.tile([P, N // P, Z_COLS], F32, name=f"yb{h}")
+        for h in halves:
+            gather(x_early[:, h, :], x_planes[h], x_list, x_wgt, 0)
+            codes, plane = weave_and_quantise(z_picked[:, :, h * HALF : (h + 1) * HALF], f"z{h}")
+            sums = keep.tile([P, N // P, HALF], F32, name=f"yb{h}")
             for m in range(N // P):
                 bank = psum.tile([P, BANK], F32, name="bank")
-                half, at = divmod(m * P, W_COLS)
+                cols = slice(m * P, (m + 1) * P)
                 for part in range(2):
-                    cols = slice(part * W_COLS + at, part * W_COLS + at + P)
                     nc.tensor.matmul_mx(
                         out=bank[:],
-                        lhsT=wb_codes[half][:, cols].bitcast(FP8X4),
-                        lhsT_scale=wb_plane[half][:, cols],
+                        lhsT=wb_mx[part][0][:, cols].bitcast(FP8X4),
+                        lhsT_scale=wb_mx[part][1][:, cols],
                         rhs=codes[:].bitcast(FP8X4),
                         rhs_scale=plane[:],
                         start=(part == 0),
@@ -141,19 +180,25 @@ def tile_list_hl_mul_gelu_kernel(
                 nc.scalar.copy(sums[:, m, :], bank[:])
             yb.append(sums)
 
-        gather(x_picked, x_planes, x_list, x_wgt, 2, 0, J)
-        chunks = J // X_COLS
+        gather(x_early[:, 2, :], x_planes[2], x_list, x_wgt, 0)
+        starts = [sum(CHUNKS[:c]) for c in range(len(CHUNKS))]
         out_rows = out.rearrange("(m p) j -> p m j", p=P)
-        per_bank = BANK // X_COLS
         ready = {}
+
+        def picked_x(c):
+            if starts[c] < X_EARLY:
+                return x_early[:, :, starts[c] : starts[c] + CHUNKS[c]]
+            return x_late[:, :, starts[c] - X_EARLY : starts[c] - X_EARLY + CHUNKS[c]]
 
         def finish(c):
             codes, plane = ready[c]
-            half, at = divmod(c * X_COLS, Z_COLS)
-            for pair in range(N // P // per_bank):
-                bank = psum.tile([P, per_bank, X_COLS], F32, name="bank")
+            cols = CHUNKS[c]
+            per_bank = BANK // cols
+            half, at = divmod(starts[c], HALF)
+            for first in range(0, N // P, per_bank):
+                bank = psum.tile([P, per_bank, cols], F32, name="bank")
                 for u in range(per_bank):
-                    m = pair * per_bank + u
+                    m = first + u
                     nc.tensor.matmul_mx(
                         out=bank[:, u, :],
                         lhsT=wa_codes[:, m * P : (m + 1) * P].bitcast(FP8X4),
@@ -163,21 +208,21 @@ def tile_list_hl_mul_gelu_kernel(
                         start=True,
                         stop=True,
                     )
-                rows = slice(pair * per_bank, (pair + 1) * per_bank)
-                product = ring.tile([P, per_bank, X_COLS], F32, name="product")
-                result = ring.tile([P, per_bank, X_COLS], F32, name="result")
-                nc.vector.tensor_tensor(product[:], bank[:], yb[half][:, rows, at : at + X_COLS], ALU.mult)
+                rows = slice(first, first + per_bank)
+                product = ring.tile([P, per_bank, cols], F32, name="product")
+                result = ring.tile([P, per_bank, cols], F32, name="result")
+                nc.vector.tensor_tensor(product[:], bank[:], yb[half][:, rows, at : at + cols], ALU.mult)
                 for u in range(per_bank):
-                    m = pair * per_bank + u
+                    m = first + u
                     nc.scalar.activation(result[:, u, :], product[:, u, :], GELU, bias=bias[:, m : m + 1])
-                nc.sync.dma_start(out_rows[:, rows, c * X_COLS : (c + 1) * X_COLS], result[:])
+                nc.sync.dma_start(out_rows[:, rows, starts[c] : starts[c] + cols], result[:])
 
-        for c in range(chunks):
-            gather(x_picked, x_planes, x_list, x_wgt, PACK - 1, c * X_COLS, X_COLS)
-            if c >= 1:
-                ready[c - 1] = quantise(x_picked, (c - 1) * X_COLS, X_COLS, f"x{c - 1}")
-            if c >= 2:
-                finish(c - 2)
-        ready[chunks - 1] = quantise(x_picked, (chunks - 1) * X_COLS, X_COLS, f"x{chunks - 1}")
-        finish(chunks - 2)
-        finish(chunks - 1)
+        for c in range(len(CHUNKS)):
+            if starts[c] == X_EARLY:
+                for i in range(PACK - 1):
+                    gather(x_late[:, i, :], x_planes[i], x_list, x_wgt, X_EARLY)
+            gather(picked_x(c)[:, PACK - 1, :], x_planes[PACK - 1], x_list, x_wgt, starts[c])
+        for c in range(len(CHUNKS)):
+            ready[c] = weave_and_quantise(picked_x(c), f"x{c}")
+        for c in range(len(CHUNKS)):
+            finish(c)

from contextlib import ExitStack

import concourse.mybir as mybir
from concourse.masks import make_identity

K, L, N, T, J = 512, 512, 512, 2048, 1024
FLOPS = 2 * (K + 2 * L) * N * J

F32 = mybir.dt.float32
BF16 = mybir.dt.bfloat16
I32 = mybir.dt.int32
U32 = mybir.dt.uint32
U16 = mybir.dt.uint16
U8 = mybir.dt.uint8
FP8X4 = mybir.dt.float8_e4m3fn_x4
ALU = mybir.AluOpType
COPY = mybir.ActivationFunctionType.Copy
GELU = mybir.ActivationFunctionType.Gelu_apprx_tanh

P = 128
PACK = 4
GROUP = 16
BANK = 512
HI_MASK = -(1 << 20)
SIGN_BIT = -(1 << 31)
W_COLS = 256
HALF = 512
CHUNKS = [512,256,256]
Z_FIRST = 896
X_EARLY = 768


def weave(engine_copy, woven, planes):
    engine_copy(
        woven.rearrange("p (c i) t -> p c t i", i=4),
        planes.rearrange("p t (c i) -> p c t i", i=4),
    )


def tile_list_hl_mul_gelu_kernel(
    tc, xT, wgt, zT, wgt2, wa_words, wa_scales, wb, b, offs, offs2, out
):
    nc = tc.nc
    with ExitStack() as ctx:
        keep = ctx.enter_context(tc.tile_pool(name="keep", bufs=1))
        ring = ctx.enter_context(tc.tile_pool(name="ring", bufs=8))
        psum = ctx.enter_context(tc.psum_pool(name="psum", bufs=8))

        x_list = keep.tile([P, J // GROUP], U16, name="x_list")
        z_list = keep.tile([P, J // GROUP], U16, name="z_list")
        x_wgt = keep.tile([P, J], F32, name="x_wgt")
        z_wgt = keep.tile([P, J], F32, name="z_wgt")
        x_planes = [keep.tile([P, T], F32, name=f"x_plane{i}") for i in range(PACK)]
        z_planes = [keep.tile([P, T], F32, name=f"z_plane{i}", align_bytes=64) for i in range(PACK)]
        wb_raw = [keep.tile([P, PACK, W_COLS], F32, name=f"wb_raw{h}") for h in range(N // W_COLS)]
        wa_codes = keep.tile([P, N], U32, name="wa_codes", align_bytes=64)
        wa_plane = keep.tile([P, N], U8, name="wa_plane", align_bytes=64)
        bias = keep.tile([P, N // P], F32, name="bias")

        identity = keep.tile([P, P], F32, name="identity")
        make_identity(nc, identity[:])
        nc.gpsimd.memset(wa_plane[:].bitcast(I32), 0)
        warm = keep.tile([P, 1], F32, name="warm")
        warm_out = keep.tile([P, 1], F32, name="warm_out")
        nc.gpsimd.memset(warm[:], 0.0)
        nc.scalar.activation(warm_out[:], warm[:], GELU)

        xT_planes = xT.rearrange("(p i) t -> p i t", i=PACK)
        zT_planes = zT.rearrange("(p i) t -> p i t", i=PACK)
        wb_planes = wb.rearrange("(p i) n -> p i n", i=PACK)
        for h in range(N // W_COLS):
            nc.sync.dma_start(wb_raw[h][:], wb_planes[:, :, h * W_COLS : (h + 1) * W_COLS])
        nc.sync.dma_start(z_list[:], offs2)
        nc.sync.dma_start(z_wgt[:, :Z_FIRST], wgt2[:, :Z_FIRST])
        for i in range(PACK):
            nc.sync.dma_start(z_planes[i][:], zT_planes[:, i, :])
        nc.sync.dma_start(z_wgt[:, Z_FIRST:], wgt2[:, Z_FIRST:])
        nc.sync.dma_start(x_list[:], offs)
        nc.sync.dma_start(x_wgt[:, :X_EARLY], wgt[:, :X_EARLY])
        for i in range(PACK):
            nc.sync.dma_start(x_planes[i][:], xT_planes[:, i, :])
        nc.sync.dma_start(x_wgt[:, X_EARLY:], wgt[:, X_EARLY:])
        nc.sync.dma_start(wa_codes[:].bitcast(I32), wa_words[0].rearrange("p n i -> p (n i)").bitcast(I32))
        scale_rows = wa_scales[0].bitcast(I32)
        for q in range(4):
            nc.sync.dma_start(wa_plane[32 * q : 32 * q + 4, :].bitcast(I32), scale_rows[4 * q : 4 * q + 4, :])
        with nc.allow_non_contiguous_dma(reason="one bias value a partition"):
            nc.sync.dma_start(bias[:], b.rearrange("(m p) -> p m", p=P))

        def quantise(woven, tag, slot=None):
            words = woven.shape[1] // PACK
            codes = keep.tile([P, words], U32, name=f"codes_{tag}", tag=slot or f"codes_{tag}", align_bytes=64)
            plane = keep.tile([P, words], U8, name=f"plane_{tag}", align_bytes=64)
            nc.vector.quantize_mx(out=codes[:].bitcast(FP8X4), scales=plane[:], in_=woven)
            return codes, plane

        hi_woven = keep.tile([P, N, PACK], BF16, name="hi_woven", align_bytes=64)
        lo_woven = keep.tile([P, N, PACK], BF16, name="lo_woven", align_bytes=64)
        minus_hi = []
        for h in range(N // W_COLS):
            negated = keep.tile([P, PACK, W_COLS], F32, name=f"minus_hi{h}")
            nc.vector.tensor_scalar(
                negated[:].bitcast(I32), wb_raw[h][:].bitcast(I32), HI_MASK, SIGN_BIT, ALU.bitwise_and, ALU.bitwise_xor
            )
            weave(
                lambda woven, planes: nc.scalar.activation(woven, planes, COPY, scale=-1.0),
                hi_woven[:, h * W_COLS : (h + 1) * W_COLS, :],
                negated[:],
            )
            minus_hi.append(negated)
        wb_mx = [quantise(hi_woven[:].rearrange("p n t -> p (n t)"), "hi")]
        lo_words = lo_woven[:].rearrange("p n t -> p (n t)").bitcast(F32).rearrange("p (n u) -> p n u", u=2)
        for h in range(N // W_COLS):
            turned = []
            for at in range(0, W_COLS, P):
                bank = psum.tile([P, PACK, P], F32, name="bank")
                for i in range(PACK):
                    for term, first in ((wb_raw[h], True), (minus_hi[h], False)):
                        nc.tensor.matmul(
                            bank[:, i, :], term[:, i, at : at + P], identity[:],
                            start=first, stop=not first, is_transpose=True,
                        )
                pairs = keep.tile([P, 2, P, 2], BF16, name=f"lo_turned{h}_{at}")
                nc.scalar.copy(pairs[:], bank[:].rearrange("n (u e) p -> n u p e", e=2))
                turned.append(pairs)
            bank = psum.tile([P, W_COLS // P, 2, P], F32, name="bank")
            for block, pairs in enumerate(turned):
                words = pairs[:].rearrange("n u p e -> n (u p e)").bitcast(F32)
                for u in range(2):
                    nc.tensor.transpose(bank[:, block, u, :], words[:, u * P : (u + 1) * P], identity[:])
            nc.scalar.copy(
                lo_words[:, h * W_COLS : (h + 1) * W_COLS, :].rearrange("p (m n) u -> p m n u", n=P),
                bank[:].rearrange("p m u n -> p m n u"),
            )

        def gather(picked, plane, lists, weights, start):
            cols = picked.shape[1]
            nc.vector.tensor_tensor(
                picked,
                plane[:].indirect(lists[:, start // GROUP : (start + cols) // GROUP]),
                weights[:, start : start + cols],
                ALU.mult,
            )

        def weave_and_quantise(picked, tag):
            woven = keep.tile([P, picked.shape[2], PACK], BF16, name=f"woven_{tag}", align_bytes=64)
            weave(nc.scalar.copy, woven[:], picked)
            return quantise(woven[:].rearrange("p j t -> p (j t)"), tag)

        halves = range(J // HALF)
        z_picked = keep.tile([P, PACK, J], F32, name="z_picked")
        x_early = keep.tile([P, PACK, X_EARLY], F32, name="x_early")
        x_late = keep.tile([P, PACK, J - X_EARLY], F32, name="x_late")
        for i in range(PACK - 1):
            gather(z_picked[:, i, :Z_FIRST], z_planes[i], z_list, z_wgt, 0)
        gather(z_picked[:, PACK - 1, :HALF], z_planes[PACK - 1], z_list, z_wgt, 0)
        for i in range(PACK - 1):
            gather(z_picked[:, i, Z_FIRST:], z_planes[i], z_list, z_wgt, Z_FIRST)
        gather(z_picked[:, PACK - 1, HALF:], z_planes[PACK - 1], z_list, z_wgt, HALF)
        wb_mx.append(quantise(lo_woven[:].rearrange("p n t -> p (n t)"), "lo", "z_plane0"))

        yb = []
        for h in halves:
            gather(x_early[:, h, :], x_planes[h], x_list, x_wgt, 0)
            codes, plane = weave_and_quantise(z_picked[:, :, h * HALF : (h + 1) * HALF], f"z{h}")
            sums = keep.tile([P, N // P, HALF], F32, name=f"yb{h}")
            for m in range(N // P):
                bank = psum.tile([P, BANK], F32, name="bank")
                cols = slice(m * P, (m + 1) * P)
                for part in range(2):
                    nc.tensor.matmul_mx(
                        out=bank[:],
                        lhsT=wb_mx[part][0][:, cols].bitcast(FP8X4),
                        lhsT_scale=wb_mx[part][1][:, cols],
                        rhs=codes[:].bitcast(FP8X4),
                        rhs_scale=plane[:],
                        start=(part == 0),
                        stop=(part == 1),
                    )
                nc.scalar.copy(sums[:, m, :], bank[:])
            yb.append(sums)

        gather(x_early[:, 2, :], x_planes[2], x_list, x_wgt, 0)
        starts = [sum(CHUNKS[:c]) for c in range(len(CHUNKS))]
        out_rows = out.rearrange("(m p) j -> p m j", p=P)
        ready = {}

        def picked_x(c):
            if starts[c] < X_EARLY:
                return x_early[:, :, starts[c] : starts[c] + CHUNKS[c]]
            return x_late[:, :, starts[c] - X_EARLY : starts[c] - X_EARLY + CHUNKS[c]]

        def finish(c):
            codes, plane = ready[c]
            cols = CHUNKS[c]
            per_bank = BANK // cols
            half, at = divmod(starts[c], HALF)
            for first in range(0, N // P, per_bank):
                bank = psum.tile([P, per_bank, cols], F32, name="bank")
                for u in range(per_bank):
                    m = first + u
                    nc.tensor.matmul_mx(
                        out=bank[:, u, :],
                        lhsT=wa_codes[:, m * P : (m + 1) * P].bitcast(FP8X4),
                        lhsT_scale=wa_plane[:, m * P : (m + 1) * P],
                        rhs=codes[:].bitcast(FP8X4),
                        rhs_scale=plane[:],
                        start=True,
                        stop=True,
                    )
                rows = slice(first, first + per_bank)
                product = ring.tile([P, per_bank, cols], F32, name="product")
                result = ring.tile([P, per_bank, cols], F32, name="result")
                nc.vector.tensor_tensor(product[:], bank[:], yb[half][:, rows, at : at + cols], ALU.mult)
                for u in range(per_bank):
                    m = first + u
                    nc.scalar.activation(result[:, u, :], product[:, u, :], GELU, bias=bias[:, m : m + 1])
                nc.sync.dma_start(out_rows[:, rows, starts[c] : starts[c] + cols], result[:])

        for c in range(len(CHUNKS)):
            if starts[c] == X_EARLY:
                for i in range(PACK - 1):
                    gather(x_late[:, i, :], x_planes[i], x_list, x_wgt, X_EARLY)
            gather(picked_x(c)[:, PACK - 1, :], x_planes[PACK - 1], x_list, x_wgt, starts[c])
        for c in range(len(CHUNKS)):
            ready[c] = weave_and_quantise(picked_x(c), f"x{c}")
        for c in range(len(CHUNKS)):
            finish(c)
